import numpy as np
import ml_dtypes


def mxq(x, axis, fmt="e4m3"):
    dtype, down = {"e4m3": (ml_dtypes.float8_e4m3fn, 7), "e5m2": (ml_dtypes.float8_e5m2, 14)}[fmt]
    v = np.moveaxis(np.asarray(x, np.float32).astype(ml_dtypes.bfloat16).astype(np.float64), axis, -1)
    blocks = v.reshape(v.shape[:-1] + (-1, 32))
    amax = np.abs(blocks).max(-1, keepdims=True)
    byte = np.maximum(np.where(amax > 0, np.frexp(amax)[1] - 1 + 127, 0) - down, 1)
    scale = np.exp2(byte - 127.0)
    codes = (blocks / scale).astype(np.float32).astype(dtype).astype(np.float64)
    return np.moveaxis((codes * scale).reshape(v.shape), -1, axis)


WIDE = False


def mx_kscale(k):
    if not WIDE:
        return np.ones(k)
    levels = np.array([10, -10, 5, -5, 0])
    if k % 512:
        return np.exp2(np.random.permutation(np.resize(levels, k // 32))).repeat(32)
    a = np.empty((k // 512, 16))
    for p in range(k // 512):
        a[p, :8] = np.random.permutation(np.resize(levels, 8))
        for g in range(8):
            far = levels[np.abs(levels - a[p, g]) >= 10]
            a[p, g + 8] = far[np.random.randint(len(far))]
    return np.exp2(a.ravel()).repeat(32)


def f64(x):
    return np.asarray(x).astype(np.float64)


def striped(idx):
    return np.tile(idx.reshape(-1, 16).T, (8, 1)).astype(np.uint16)


def unstriped(offs):
    return offs[:16].T.reshape(-1).astype(np.int64)


E2M1 = np.array([0.0, 0.5, 1.0, 1.5, 2.0, 3.0, 4.0, 6.0, -0.0, -0.5, -1.0, -1.5, -2.0, -3.0, -4.0, -6.0])


def pack_weight(w, fmt):
    k, n = w.shape
    w = f64(np.asarray(w, np.float32).astype(ml_dtypes.bfloat16)).reshape(k // 32, 32, n)
    amax = np.abs(w).max(1)
    if fmt == "e4m3":
        byte = np.frexp(amax)[1] - 1 + 127 - 7
    else:
        mant, ex = np.frexp(amax / 6.0)
        byte = np.where(mant > 0.5, ex, ex - 1) + 127
    byte = np.clip(np.where(amax > 0, byte, 1), 1, 254)
    scaled = (w * np.exp2(127.0 - byte)[:, None, :]).reshape(k, n).astype(np.float32)
    by_word = np.ascontiguousarray(scaled.reshape(k // 512, 128, 4, n).transpose(0, 1, 3, 2))
    if fmt == "e4m3":
        words = by_word.astype(ml_dtypes.float8_e4m3fn).view(np.uint8)
    else:
        c = by_word.astype(ml_dtypes.float4_e2m1fn).view(np.uint8) & 0xF
        words = (c[..., 0::2] | (c[..., 1::2] << 4)).reshape(k // 512, 128, 2 * n)
    return np.ascontiguousarray(words), np.ascontiguousarray(byte.astype(np.uint8).reshape(k // 512, 16, n))


def unpack_weight(words, scales, fmt):
    g, _, n = scales.shape
    words = np.ascontiguousarray(words).reshape(g, 128, n, -1)
    if fmt == "e4m3":
        vals = words.view(ml_dtypes.float8_e4m3fn).astype(np.float64)
    else:
        nib = np.empty((g, 128, n, 4), np.uint8)
        nib[..., 0::2] = words & 0xF
        nib[..., 1::2] = words >> 4
        vals = E2M1[nib]
    vals = vals * np.repeat(np.exp2(scales.astype(np.float64) - 127.0), 8, axis=1)[..., None]
    return vals.transpose(0, 1, 3, 2).reshape(g * 512, n)


def gelu(v):
    return 0.5 * v * (1.0 + np.tanh(np.sqrt(2.0 / np.pi) * (v + 0.044715 * v**3)))


K, T, S, H, P, N = 1024, 4096, 1024, 1024, 512, 768

def setup_inputs():
    n = np.random.standard_normal
    s = mx_kscale(K)[:, None]
    u = mx_kscale(H)[:, None]
    d = {}
    d["tab_words"], d["tab_scales"] = pack_weight(n((K, T)) * s, "e2m1")
    d["offs"] = striped(np.random.permutation(T)[:S])
    perm = np.random.permutation(S)
    d["pos1"] = striped(perm[:P])
    d["pos2"] = striped(perm[P:2 * P])
    d["w1"] = (n((K, H)) / K**0.5 / s * u.T).astype(np.float32)
    d["b1"] = (0.6 * n(H) * u[:, 0]).astype(np.float32)
    d["w2_words"], d["w2_scales"] = pack_weight(n((H, N)) / H**0.5 / u, "e2m1")
    d["w3"] = (n((H, N)) / H**0.5 / u).astype(np.float32)
    d["b3"] = (0.6 * n(N)).astype(np.float32)
    return d

def reference(tab_words, tab_scales, offs, pos1, pos2, w1, b1, w2_words, w2_scales, w3, b3):
    v = unpack_weight(tab_words, tab_scales, "e2m1")[:, unstriped(offs)]
    h = (mxq(f64(w1), 0, "e4m3").T @ v) + f64(b1)[:, None]
    first = h[:, unstriped(pos1)]
    second = h[:, unstriped(pos2)]
    gap = mxq(first - second, 0, "e4m3")
    peak = mxq(np.maximum(first, second), 0, "e4m3")
    w2 = unpack_weight(w2_words, w2_scales, "e2m1")
    y = w2.T @ gap
    load = (mxq(f64(w3), 0, "e4m3").T @ peak) + f64(b3)[:, None]
    return y * np.tanh(load)

@@ -1,0 +1,262 @@
+from contextlib import ExitStack
+
+import concourse.mybir as mybir
+
+K, T, S, H, PAIRS, N = 1024, 4096, 1024, 1024, 512, 768
+FLOPS = 2 * K * H * S + 2 * 2 * H * N * PAIRS
+
+F32 = mybir.dt.float32
+BF16 = mybir.dt.bfloat16
+I32 = mybir.dt.int32
+U32 = mybir.dt.uint32
+U16 = mybir.dt.uint16
+U8 = mybir.dt.uint8
+FP8X4 = mybir.dt.float8_e4m3fn_x4
+FP4X4 = mybir.dt.float4_e2m1fn_x4
+ACT = mybir.ActivationFunctionType
+ALU = mybir.AluOpType
+
+P = 128
+PACK = 4
+KP = P * PACK
+BANK = 512
+AL = 64
+PIECES = ((0, 256), (256, 256))
+
+
+def tile_list_sector_encounter_complexity_kernel(
+    tc, tab_words, tab_scales, offs, pos1, pos2, w1, b1, w2_words, w2_scales, w3, b3, out
+):
+    nc = tc.nc
+    with ExitStack() as ctx:
+        lists = ctx.enter_context(tc.tile_pool(name="lists", bufs=1))
+        keep = ctx.enter_context(tc.tile_pool(name="keep", bufs=1))
+        psum = ctx.enter_context(tc.psum_pool(name="psum", bufs=1))
+
+        def sb(shape, dtype, name, tag=None):
+            return keep.tile(shape, dtype, name=name, tag=tag or name, align_bytes=AL)
+
+        def bank(i, name):
+            return psum.tile([P, BANK], F32, name=name, tag="bank%d" % (i % 8))
+
+        offs_sb = lists.tile([P, S // 16], U16, name="offs_sb")
+        pos1_sb = lists.tile([P, PAIRS // 16], U16, name="pos1_sb")
+        pos2_sb = lists.tile([P, PAIRS // 16], U16, name="pos2_sb")
+
+        tab_s = sb([P, T], U8, "tab_s")
+        nc.vector.memset(tab_s[:].bitcast(I32), 0)
+        warm_in = sb([P, 1], F32, "warm_in", "tab_w1")
+        warm_bias = sb([P, 1], F32, "warm_bias", "stage_c")
+        warm_out = sb([P, 1], F32, "warm_out", "stage_b")
+        nc.vector.memset(warm_in[:], 0.0)
+        nc.vector.memset(warm_bias[:], 0.0)
+        v_scale1 = sb([P, S], U8, "v_scale1")
+        nc.vector.memset(v_scale1[:].bitcast(I32), 0)
+
+        nc.sync.dma_start(offs_sb[:], offs)
+        tab_w = [sb([P, T], U16, "tab_w0")]
+        nc.sync.dma_start(tab_w[0][:].bitcast(I32), tab_words[0].bitcast(I32))
+        rows = tab_scales.bitcast(I32).rearrange("a (q r) c -> r q a c", r=4)
+        for r in range(4):
+            nc.scalar.dma_start(tab_s[:].bitcast(I32)[r:P:16, :], rows[r])
+        nc.scalar.activation(warm_out[:], warm_in[:], ACT.Tanh, bias=warm_bias[:])
+
+        def load_w1(b, a, c0, width, tag):
+            raw = sb([P, PACK, width], F32, "w1raw_%d%d_%d" % (b, a, c0), tag)
+            src = w1[KP * a : KP * (a + 1), KP * b + c0 : KP * b + c0 + width]
+            nc.sync.dma_start(raw[:], src.rearrange("(p j) c -> p j c", j=PACK))
+            return raw
+
+        def cast_w1(copy, raw, grouped, c0, width):
+            q0, nq = c0 // PACK, width // PACK
+            dst = grouped[:].rearrange("p (u e q j) -> p q u j e", u=2, e=2, j=PACK)[:, q0 : q0 + nq]
+            copy(dst, raw[:].rearrange("p j (q u e) -> p q u j e", u=2, e=2))
+
+        def quantize(grouped, codes, scales, widths):
+            c = 0
+            for w in widths:
+                nc.vector.quantize_mx(
+                    out=codes[:, c : c + w].bitcast(FP8X4),
+                    scales=scales[:, c : c + w],
+                    in_=grouped[:, PACK * c : PACK * (c + w)],
+                )
+                c = c + w
+
+        raw00 = load_w1(0, 0, 0, KP, "stage_a")
+        tab_w.append(sb([P, T], U16, "tab_w1"))
+        nc.sync.dma_start(tab_w[1][:].bitcast(I32), tab_words[1].bitcast(I32))
+        raw01l = load_w1(0, 1, 0, KP // 2, "stage_b")
+        raw01r = load_w1(0, 1, KP // 2, KP // 2, "stage_c")
+        b1_sb = sb([P, 2, PACK], F32, "b1_sb")
+        nc.sync.dma_start(b1_sb[:], b1.rearrange("(b p t) -> p b t", p=P, t=PACK))
+        nc.sync.dma_start(pos1_sb[:], pos1)
+        nc.sync.dma_start(pos2_sb[:], pos2)
+
+        v_words = [sb([P, S], U16, "v_words%d" % a) for a in range(2)]
+        v_scale0 = sb([P, S], U8, "v_scale0")
+        nc.vector.tensor_copy(v_words[0][:], tab_w[0][:].indirect(offs_sb[:]))
+        nc.vector.tensor_copy(v_scale0[:], tab_s[:].indirect(offs_sb[:]))
+        nc.vector.tensor_copy(v_words[1][:], tab_w[1][:].indirect(offs_sb[:]))
+        nc.sync.dma_start(v_scale1[:].bitcast(I32)[0 : P - 16, :], v_scale0[:].bitcast(I32)[16:P, :])
+        v_scales = [v_scale0, v_scale1]
+
+        w1_codes = [[sb([P, KP], U32, "w1c%d%d" % (b, a)) for a in range(2)] for b in range(2)]
+        w1_scales = [[sb([P, KP], U8, "w1s%d%d" % (b, a)) for a in range(2)] for b in range(2)]
+        h = [[sb([P, S], F32, "h%d%d" % (b, t)) for t in range(PACK)] for b in range(2)]
+
+        g00 = sb([P, KP * PACK], BF16, "g00", "grp_a")
+        cast_w1(nc.scalar.copy, raw00, g00, 0, KP)
+        quantize(g00, w1_codes[0][0], w1_scales[0][0], [KP])
+        g01 = sb([P, KP * PACK], BF16, "g01", "grp_b")
+        cast_w1(nc.scalar.copy, raw01l, g01, 0, KP // 2)
+        cast_w1(nc.vector.tensor_copy, raw01r, g01, KP // 2, KP // 2)
+        quantize(g01, w1_codes[0][1], w1_scales[0][1], [P] * PACK)
+
+        def stage1(b, t):
+            banks = [bank(2 * t + m, "acc%d%d%d" % (b, t, m)) for m in range(2)]
+            for a in range(2):
+                for m in range(2):
+                    cols = slice(BANK * m, BANK * (m + 1))
+                    nc.tensor.matmul_mx(
+                        out=banks[m][:],
+                        lhsT=w1_codes[b][a][:, P * t : P * (t + 1)].bitcast(FP8X4),
+                        lhsT_scale=w1_scales[b][a][:, P * t : P * (t + 1)],
+                        rhs=v_words[a][:, cols].bitcast(FP4X4),
+                        rhs_scale=v_scales[a][:, cols],
+                        start=(a == 0),
+                        stop=(a == 1),
+                    )
+            for m in range(2):
+                cols = slice(BANK * m, BANK * (m + 1))
+                bias = b1_sb[:, b, t : t + 1]
+                if (b, t, m) == (0, 0, 1):
+                    nc.vector.tensor_scalar(h[b][t][:, cols], banks[m][:], bias, None, ALU.add)
+                else:
+                    nc.scalar.activation(h[b][t][:, cols], banks[m][:], ACT.Identity, bias=bias)
+
+        def pick(b, t, first, second, j0, w):
+            cols = slice(j0 // 16, (j0 + w) // 16)
+            nc.vector.tensor_copy(first[:, t, :], h[b][t][:].indirect(pos1_sb[:, cols]))
+            nc.vector.tensor_copy(second[:, t, :], h[b][t][:].indirect(pos2_sb[:, cols]))
+
+        def combine(b, first, second, j0, w):
+            made = []
+            for op, nm in ((ALU.max, "peak"), (ALU.subtract, "gap")):
+                g = sb([P, w * PACK], BF16, "%s_bf%d_%d" % (nm, b, j0), {"peak": "grp_b", "gap": "gap_bf"}[nm])
+                nc.vector.tensor_tensor(
+                    g[:].rearrange("p (c i t) -> p c t i", i=2, t=PACK),
+                    first[:].rearrange("p t (c i) -> p c t i", i=2),
+                    second[:].rearrange("p t (c i) -> p c t i", i=2),
+                    op,
+                )
+                made.append((nm, g))
+            res = {}
+            for nm, g in made:
+                codes = sb([P, w], U32, "%s_c%d_%d" % (nm, b, j0))
+                scales = sb([P, w], U8, "%s_s%d_%d" % (nm, b, j0))
+                quantize(g, codes, scales, [w])
+                res[nm] = (codes, scales)
+            return res
+
+        first0 = sb([P, PACK, PAIRS], F32, "first0", "first")
+        second0 = sb([P, PACK, PAIRS], F32, "second0", "second")
+        for t in range(2):
+            stage1(0, t)
+            pick(0, t, first0, second0, 0, PAIRS)
+        raw10 = load_w1(1, 0, 0, KP, "stage_b")
+        raw11 = load_w1(1, 1, 0, KP, "stage_c")
+        g10 = sb([P, KP * PACK], BF16, "g10", "grp_a")
+        cast_w1(nc.scalar.copy, raw10, g10, 0, KP)
+        quantize(g10, w1_codes[1][0], w1_scales[1][0], [KP])
+        for t in range(2, PACK):
+            stage1(0, t)
+            pick(0, t, first0, second0, 0, PAIRS)
+        g11 = sb([P, KP * PACK], BF16, "g11", "grp_b")
+        cast_w1(nc.scalar.copy, raw11, g11, 0, KP)
+        quantize(g11, w1_codes[1][1], w1_scales[1][1], [KP])
+        for t in range(PACK):
+            stage1(1, t)
+        ops0 = combine(0, first0, second0, 0, PAIRS)
+
+        w3_codes = [sb([P, N], U32, "w3c%d" % b) for b in range(2)]
+        w3_scales = [sb([P, N], U8, "w3s%d" % b) for b in range(2)]
+        w3_raw = []
+        for b in range(2):
+            raw = sb([P, PACK, N], F32, "w3raw%d" % b, ("stage_b", "stage_c")[b])
+            nc.sync.dma_start(raw[:], w3[KP * b : KP * (b + 1), :].rearrange("(p j) c -> p j c", j=PACK))
+            w3_raw.append(raw)
+        w2 = sb([P, 6 * N], U8, "w2", "grp_a")
+        w2w = w2[:, : 4 * N].rearrange("p (a c) -> p a c", a=2)
+        w2s = w2[:, 4 * N :].rearrange("p (a c) -> p a c", a=2)
+        nc.sync.dma_start(w2w.bitcast(I32), w2_words.bitcast(I32).rearrange("a p c -> p a c"))
+        nc.gpsimd.memset(w2[:, 4 * N :].bitcast(I32), 0)
+        rows2 = w2_scales.bitcast(I32).rearrange("a (q r) c -> r q a c", r=4)
+        for r in range(4):
+            nc.sync.dma_start(w2s.bitcast(I32)[r:P:32, :, :], rows2[r])
+        b3_sb = sb([P, N // P], F32, "b3_sb", "stage_a")
+        with nc.allow_non_contiguous_dma(reason="one bias value for each partition"):
+            nc.sync.dma_start(b3_sb[:], b3.rearrange("(i p) -> p i", p=P))
+        for b in range(2):
+            g3 = sb([P, N * PACK], BF16, "g3_%d" % b)
+            for c0, w in ((0, 512), (512, 256)):
+                nc.scalar.copy(
+                    g3[:, PACK * c0 : PACK * (c0 + w)].rearrange("p (c i j) -> p c j i", i=2, j=PACK),
+                    w3_raw[b][:, :, c0 : c0 + w].rearrange("p j (c i) -> p c j i", i=2),
+                )
+            quantize(g3, w3_codes[b], w3_scales[b], [512, 256])
+
+        out_v = out.rearrange("(i p) j -> p i j", p=P)
+        nb = 0
+        for j0, w in PIECES:
+            first1 = sb([P, PACK, w], F32, "first1_%d" % j0, "first")
+            second1 = sb([P, PACK, w], F32, "second1_%d" % j0, "second")
+            for t in range(PACK):
+                pick(1, t, first1, second1, j0, w)
+            ops1 = combine(1, first1, second1, j0, w)
+            per = 2 if w == 256 else 3
+            groups = list(range(0, N // P, per))
+            load_b = {}
+            y_b = {}
+            for i0 in groups:
+                load_b[i0] = bank(nb, "load%d_%d" % (j0, i0))
+                y_b[i0] = bank(nb + 1, "y%d_%d" % (j0, i0))
+                nb = nb + 2
+            for b, ops, c0 in ((0, ops0, j0), (1, ops1, 0)):
+                for i0 in groups:
+                    codes, scales = ops["peak"]
+                    for k in range(per):
+                        i = i0 + k
+                        nc.tensor.matmul_mx(
+                            out=load_b[i0][:, w * k : w * (k + 1)],
+                            lhsT=w3_codes[b][:, P * i : P * (i + 1)].bitcast(FP8X4),
+                            lhsT_scale=w3_scales[b][:, P * i : P * (i + 1)],
+                            rhs=codes[:, c0 : c0 + w].bitcast(FP8X4),
+                            rhs_scale=scales[:, c0 : c0 + w],
+                            start=(b == 0 and k == 0),
+                            stop=(b == 1 and k == per - 1),
+                        )
+                    codes, scales = ops["gap"]
+                    for k in range(per):
+                        i = i0 + k
+                        for s0 in range(0, w, P):
+                            nc.tensor.matmul_mx(
+                                out=y_b[i0][:, w * k + s0 : w * k + s0 + P],
+                                lhsT=w2w[:, b, 2 * P * i : 2 * P * (i + 1)].bitcast(FP4X4),
+                                lhsT_scale=w2s[:, b, P * i : P * (i + 1)],
+                                rhs=codes[:, c0 + s0 : c0 + s0 + P].bitcast(FP8X4),
+                                rhs_scale=scales[:, c0 + s0 : c0 + s0 + P],
+                                start=(b == 0 and k == 0 and s0 == 0),
+                                stop=(b == 1 and k == per - 1 and s0 == w - P),
+                            )
+            for i0 in groups:
+                th = sb([P, per * w], F32, "th%d_%d" % (j0, i0))
+                for k in range(per):
+                    cols = slice(w * k, w * (k + 1))
+                    nc.scalar.activation(
+                        th[:, cols], load_b[i0][:, cols], ACT.Tanh, bias=b3_sb[:, i0 + k : i0 + k + 1]
+                    )
+                res = sb([P, per * w], F32, "res%d_%d" % (j0, i0))
+                nc.vector.tensor_tensor(res[:], y_b[i0][:, : per * w], th[:], ALU.mult)
+                nc.sync.dma_start(
+                    out_v[:, i0 : i0 + per, j0 : j0 + w], res[:].rearrange("p (k j) -> p k j", k=per)
+                )

@@ -21,7 +21,6 @@ PACK = 4
 KP = P * PACK
 BANK = 512
 AL = 64
-PIECES = ((0, 256), (256, 256))
 
 
 def tile_list_sector_encounter_complexity_kernel(
@@ -46,8 +45,8 @@ def tile_list_sector_encounter_complexity_kernel(
         tab_s = sb([P, T], U8, "tab_s")
         nc.vector.memset(tab_s[:].bitcast(I32), 0)
         warm_in = sb([P, 1], F32, "warm_in", "tab_w1")
-        warm_bias = sb([P, 1], F32, "warm_bias", "stage_c")
         warm_out = sb([P, 1], F32, "warm_out", "stage_b")
+        warm_bias = sb([P, 1], F32, "warm_bias", "stage_a")
         nc.vector.memset(warm_in[:], 0.0)
         nc.vector.memset(warm_bias[:], 0.0)
         v_scale1 = sb([P, S], U8, "v_scale1")
@@ -61,16 +60,17 @@ def tile_list_sector_encounter_complexity_kernel(
             nc.scalar.dma_start(tab_s[:].bitcast(I32)[r:P:16, :], rows[r])
         nc.scalar.activation(warm_out[:], warm_in[:], ACT.Tanh, bias=warm_bias[:])
 
-        def load_w1(b, a, c0, width, tag):
-            raw = sb([P, PACK, width], F32, "w1raw_%d%d_%d" % (b, a, c0), tag)
-            src = w1[KP * a : KP * (a + 1), KP * b + c0 : KP * b + c0 + width]
+        def load_w1(b, a, tag):
+            raw = sb([P, PACK, KP], F32, "w1raw_%d%d" % (b, a), tag)
+            src = w1[KP * a : KP * (a + 1), KP * b : KP * (b + 1)]
             nc.sync.dma_start(raw[:], src.rearrange("(p j) c -> p j c", j=PACK))
             return raw
 
-        def cast_w1(copy, raw, grouped, c0, width):
-            q0, nq = c0 // PACK, width // PACK
-            dst = grouped[:].rearrange("p (u e q j) -> p q u j e", u=2, e=2, j=PACK)[:, q0 : q0 + nq]
-            copy(dst, raw[:].rearrange("p j (q u e) -> p q u j e", u=2, e=2))
+        def cast_w1(raw, grouped):
+            nc.scalar.copy(
+                grouped[:].rearrange("p (u e q j) -> p q u j e", u=2, e=2, j=PACK),
+                raw[:].rearrange("p j (q u e) -> p q u j e", u=2, e=2),
+            )
 
         def quantize(grouped, codes, scales, widths):
             c = 0
@@ -82,13 +82,10 @@ def tile_list_sector_encounter_complexity_kernel(
                 )
                 c = c + w
 
-        raw00 = load_w1(0, 0, 0, KP, "stage_a")
+        raw00 = load_w1(0, 0, "stage_a")
         tab_w.append(sb([P, T], U16, "tab_w1"))
         nc.sync.dma_start(tab_w[1][:].bitcast(I32), tab_words[1].bitcast(I32))
-        raw01l = load_w1(0, 1, 0, KP // 2, "stage_b")
-        raw01r = load_w1(0, 1, KP // 2, KP // 2, "stage_c")
-        b1_sb = sb([P, 2, PACK], F32, "b1_sb")
-        nc.sync.dma_start(b1_sb[:], b1.rearrange("(b p t) -> p b t", p=P, t=PACK))
+        raw01 = load_w1(0, 1, "stage_b")
         nc.sync.dma_start(pos1_sb[:], pos1)
         nc.sync.dma_start(pos2_sb[:], pos2)
 
@@ -99,28 +96,42 @@ def tile_list_sector_encounter_complexity_kernel(
         nc.vector.tensor_copy(v_words[1][:], tab_w[1][:].indirect(offs_sb[:]))
         nc.sync.dma_start(v_scale1[:].bitcast(I32)[0 : P - 16, :], v_scale0[:].bitcast(I32)[16:P, :])
         v_scales = [v_scale0, v_scale1]
+        b1_sb = sb([P, 2, PACK], F32, "b1_sb", "tab_s")
+        nc.sync.dma_start(b1_sb[:], b1.rearrange("(b p t) -> p b t", p=P, t=PACK))
 
-        w1_codes = [[sb([P, KP], U32, "w1c%d%d" % (b, a)) for a in range(2)] for b in range(2)]
-        w1_scales = [[sb([P, KP], U8, "w1s%d%d" % (b, a)) for a in range(2)] for b in range(2)]
+        w1_q = {}
+
+        def quantize_w1(grouped, b, a, t0, widths, tag=None):
+            n = sum(widths)
+            codes = sb([P, n], U32, "w1c%d%d%d" % (b, a, t0), tag)
+            scales = sb([P, n], U8, "w1s%d%d%d" % (b, a, t0))
+            quantize(grouped, codes, scales, widths)
+            for t in range(t0, t0 + n // P):
+                cols = slice(P * (t - t0), P * (t - t0 + 1))
+                w1_q[b, a, t] = (codes[:, cols].bitcast(FP8X4), scales[:, cols])
+
         h = [[sb([P, S], F32, "h%d%d" % (b, t)) for t in range(PACK)] for b in range(2)]
 
         g00 = sb([P, KP * PACK], BF16, "g00", "grp_a")
-        cast_w1(nc.scalar.copy, raw00, g00, 0, KP)
-        quantize(g00, w1_codes[0][0], w1_scales[0][0], [KP])
-        g01 = sb([P, KP * PACK], BF16, "g01", "grp_b")
-        cast_w1(nc.scalar.copy, raw01l, g01, 0, KP // 2)
-        cast_w1(nc.vector.tensor_copy, raw01r, g01, KP // 2, KP // 2)
-        quantize(g01, w1_codes[0][1], w1_scales[0][1], [P] * PACK)
+        cast_w1(raw00, g00)
+        quantize_w1(g00, 0, 0, 0, [KP])
+        for u, copy in enumerate((nc.vector.tensor_copy, nc.scalar.copy)):
+            g01 = sb([P, KP * 2], BF16, "g01_%d" % u, ("grp_b", "grp_c")[u])
+            copy(
+                g01[:].rearrange("p (e q j) -> p q j e", e=2, j=PACK),
+                raw01[:].rearrange("p j (q u e) -> p u q j e", u=2, e=2)[:, u],
+            )
+            quantize_w1(g01, 0, 1, 2 * u, [P, P] if u == 0 else [2 * P])
 
         def stage1(b, t):
-            banks = [bank(2 * t + m, "acc%d%d%d" % (b, t, m)) for m in range(2)]
+            banks = [bank(4 * b + (2 * t + m) % 4, "acc%d%d%d" % (b, t, m)) for m in range(2)]
             for a in range(2):
                 for m in range(2):
                     cols = slice(BANK * m, BANK * (m + 1))
                     nc.tensor.matmul_mx(
                         out=banks[m][:],
-                        lhsT=w1_codes[b][a][:, P * t : P * (t + 1)].bitcast(FP8X4),
-                        lhsT_scale=w1_scales[b][a][:, P * t : P * (t + 1)],
+                        lhsT=w1_q[b, a, t][0],
+                        lhsT_scale=w1_q[b, a, t][1],
                         rhs=v_words[a][:, cols].bitcast(FP4X4),
                         rhs_scale=v_scales[a][:, cols],
                         start=(a == 0),
@@ -139,50 +150,49 @@ def tile_list_sector_encounter_complexity_kernel(
             nc.vector.tensor_copy(first[:, t, :], h[b][t][:].indirect(pos1_sb[:, cols]))
             nc.vector.tensor_copy(second[:, t, :], h[b][t][:].indirect(pos2_sb[:, cols]))
 
-        def combine(b, first, second, j0, w):
-            made = []
-            for op, nm in ((ALU.max, "peak"), (ALU.subtract, "gap")):
-                g = sb([P, w * PACK], BF16, "%s_bf%d_%d" % (nm, b, j0), {"peak": "grp_b", "gap": "gap_bf"}[nm])
+        def combine(op, first, second, g, parts):
+            w = PAIRS // parts
+            for c0 in range(0, PAIRS, w):
                 nc.vector.tensor_tensor(
-                    g[:].rearrange("p (c i t) -> p c t i", i=2, t=PACK),
-                    first[:].rearrange("p t (c i) -> p c t i", i=2),
-                    second[:].rearrange("p t (c i) -> p c t i", i=2),
+                    g[:, PACK * c0 : PACK * (c0 + w)].rearrange("p (c i t) -> p c t i", i=2, t=PACK),
+                    first[:, :, c0 : c0 + w].rearrange("p t (c i) -> p c t i", i=2),
+                    second[:, :, c0 : c0 + w].rearrange("p t (c i) -> p c t i", i=2),
                     op,
                 )
-                made.append((nm, g))
-            res = {}
-            for nm, g in made:
-                codes = sb([P, w], U32, "%s_c%d_%d" % (nm, b, j0))
-                scales = sb([P, w], U8, "%s_s%d_%d" % (nm, b, j0))
-                quantize(g, codes, scales, [w])
-                res[nm] = (codes, scales)
-            return res
+
+        def operand(name, tag=None):
+            return sb([P, PAIRS], U32, name + "_c", tag), sb([P, PAIRS], U8, name + "_s")
 
         first0 = sb([P, PACK, PAIRS], F32, "first0", "first")
         second0 = sb([P, PACK, PAIRS], F32, "second0", "second")
         for t in range(2):
             stage1(0, t)
             pick(0, t, first0, second0, 0, PAIRS)
-        raw10 = load_w1(1, 0, 0, KP, "stage_b")
-        raw11 = load_w1(1, 1, 0, KP, "stage_c")
+        raw10 = load_w1(1, 0, "stage_b")
+        raw11 = load_w1(1, 1, "grp_c")
         g10 = sb([P, KP * PACK], BF16, "g10", "grp_a")
-        cast_w1(nc.scalar.copy, raw10, g10, 0, KP)
-        quantize(g10, w1_codes[1][0], w1_scales[1][0], [KP])
+        cast_w1(raw10, g10)
+        quantize_w1(g10, 1, 0, 0, [KP])
         for t in range(2, PACK):
             stage1(0, t)
             pick(0, t, first0, second0, 0, PAIRS)
         g11 = sb([P, KP * PACK], BF16, "g11", "grp_b")
-        cast_w1(nc.scalar.copy, raw11, g11, 0, KP)
-        quantize(g11, w1_codes[1][1], w1_scales[1][1], [KP])
+        cast_w1(raw11, g11)
+        quantize_w1(g11, 1, 1, 0, [KP])
         for t in range(PACK):
             stage1(1, t)
-        ops0 = combine(0, first0, second0, 0, PAIRS)
+        peak0_bf = sb([P, PAIRS * PACK], BF16, "peak0_bf", "grp_b")
+        combine(ALU.max, first0, second0, peak0_bf, 1)
+        gap_bf = sb([P, PAIRS * PACK], BF16, "gap0_bf", "gap_bf")
+        combine(ALU.subtract, first0, second0, gap_bf, 1)
+        gap = [operand("gap0")]
+        quantize(gap_bf, gap[0][0], gap[0][1], [PAIRS])
 
         w3_codes = [sb([P, N], U32, "w3c%d" % b) for b in range(2)]
         w3_scales = [sb([P, N], U8, "w3s%d" % b) for b in range(2)]
         w3_raw = []
         for b in range(2):
-            raw = sb([P, PACK, N], F32, "w3raw%d" % b, ("stage_b", "stage_c")[b])
+            raw = sb([P, PACK, N], F32, "w3raw%d" % b, ("stage_b", "grp_c")[b])
             nc.sync.dma_start(raw[:], w3[KP * b : KP * (b + 1), :].rearrange("(p j) c -> p j c", j=PACK))
             w3_raw.append(raw)
         w2 = sb([P, 6 * N], U8, "w2", "grp_a")
@@ -193,9 +203,6 @@ def tile_list_sector_encounter_complexity_kernel(
         rows2 = w2_scales.bitcast(I32).rearrange("a (q r) c -> r q a c", r=4)
         for r in range(4):
             nc.sync.dma_start(w2s.bitcast(I32)[r:P:32, :, :], rows2[r])
-        b3_sb = sb([P, N // P], F32, "b3_sb", "stage_a")
-        with nc.allow_non_contiguous_dma(reason="one bias value for each partition"):
-            nc.sync.dma_start(b3_sb[:], b3.rearrange("(i p) -> p i", p=P))
         for b in range(2):
             g3 = sb([P, N * PACK], BF16, "g3_%d" % b)
             for c0, w in ((0, 512), (512, 256)):
@@ -205,58 +212,64 @@ def tile_list_sector_encounter_complexity_kernel(
                 )
             quantize(g3, w3_codes[b], w3_scales[b], [512, 256])
 
-        out_v = out.rearrange("(i p) j -> p i j", p=P)
-        nb = 0
-        for j0, w in PIECES:
-            first1 = sb([P, PACK, w], F32, "first1_%d" % j0, "first")
-            second1 = sb([P, PACK, w], F32, "second1_%d" % j0, "second")
-            for t in range(PACK):
-                pick(1, t, first1, second1, j0, w)
-            ops1 = combine(1, first1, second1, j0, w)
-            per = 2 if w == 256 else 3
-            groups = list(range(0, N // P, per))
-            load_b = {}
-            y_b = {}
-            for i0 in groups:
-                load_b[i0] = bank(nb, "load%d_%d" % (j0, i0))
-                y_b[i0] = bank(nb + 1, "y%d_%d" % (j0, i0))
-                nb = nb + 2
-            for b, ops, c0 in ((0, ops0, j0), (1, ops1, 0)):
-                for i0 in groups:
-                    codes, scales = ops["peak"]
-                    for k in range(per):
-                        i = i0 + k
-                        nc.tensor.matmul_mx(
-                            out=load_b[i0][:, w * k : w * (k + 1)],
-                            lhsT=w3_codes[b][:, P * i : P * (i + 1)].bitcast(FP8X4),
-                            lhsT_scale=w3_scales[b][:, P * i : P * (i + 1)],
-                            rhs=codes[:, c0 : c0 + w].bitcast(FP8X4),
-                            rhs_scale=scales[:, c0 : c0 + w],
-                            start=(b == 0 and k == 0),
-                            stop=(b == 1 and k == per - 1),
-                        )
-                    codes, scales = ops["gap"]
-                    for k in range(per):
-                        i = i0 + k
-                        for s0 in range(0, w, P):
-                            nc.tensor.matmul_mx(
-                                out=y_b[i0][:, w * k + s0 : w * k + s0 + P],
-                                lhsT=w2w[:, b, 2 * P * i : 2 * P * (i + 1)].bitcast(FP4X4),
-                                lhsT_scale=w2s[:, b, P * i : P * (i + 1)],
-                                rhs=codes[:, c0 + s0 : c0 + s0 + P].bitcast(FP8X4),
-                                rhs_scale=scales[:, c0 + s0 : c0 + s0 + P],
-                                start=(b == 0 and k == 0 and s0 == 0),
-                                stop=(b == 1 and k == per - 1 and s0 == w - P),
-                            )
-            for i0 in groups:
-                th = sb([P, per * w], F32, "th%d_%d" % (j0, i0))
-                for k in range(per):
-                    cols = slice(w * k, w * (k + 1))
-                    nc.scalar.activation(
-                        th[:, cols], load_b[i0][:, cols], ACT.Tanh, bias=b3_sb[:, i0 + k : i0 + k + 1]
-                    )
-                res = sb([P, per * w], F32, "res%d_%d" % (j0, i0))
-                nc.vector.tensor_tensor(res[:], y_b[i0][:, : per * w], th[:], ALU.mult)
-                nc.sync.dma_start(
-                    out_v[:, i0 : i0 + per, j0 : j0 + w], res[:].rearrange("p (k j) -> p k j", k=per)
-                )
+        b3_sb = sb([P, N // P], F32, "b3_sb", "stage_b")
+        with nc.allow_non_contiguous_dma(reason="one bias value for each partition"):
+            nc.sync.dma_start(b3_sb[:], b3.rearrange("(i p) -> p i", p=P))
+
+        first1 = sb([P, PACK, PAIRS], F32, "first1", "first")
+        second1 = sb([P, PACK, PAIRS], F32, "second1", "second")
+        for t in range(PACK):
+            pick(1, t, first1, second1, 0, PAIRS)
+        peak = [operand("peak0", "h13")]
+        quantize(peak0_bf, peak[0][0], peak[0][1], [PAIRS])
+        peak1_bf = sb([P, PAIRS * PACK], BF16, "peak1_bf")
+        combine(ALU.max, first1, second1, peak1_bf, 2)
+        peak.append(operand("peak1"))
+        quantize(peak1_bf, peak[1][0], peak[1][1], [PAIRS // 2] * 2)
+        gap_bf = sb([P, PAIRS * PACK], BF16, "gap1_bf", "gap_bf")
+        combine(ALU.subtract, first1, second1, gap_bf, 2)
+        gap.append(operand("gap1"))
+        quantize(gap_bf, gap[1][0], gap[1][1], [PAIRS // 2] * 2)
+
+        def load_pass(acc, i, b):
+            nc.tensor.matmul_mx(
+                out=acc[:],
+                lhsT=w3_codes[b][:, P * i : P * (i + 1)].bitcast(FP8X4),
+                lhsT_scale=w3_scales[b][:, P * i : P * (i + 1)],
+                rhs=peak[b][0][:].bitcast(FP8X4),
+                rhs_scale=peak[b][1][:],
+                start=(b == 0),
+                stop=(b == 1),
+            )
+
+        def y_pass(acc, i, b):
+            nc.tensor.matmul_mx(
+                out=acc[:],
+                lhsT=w2w[:, b, 2 * P * i : 2 * P * (i + 1)].bitcast(FP4X4),
+                lhsT_scale=w2s[:, b, P * i : P * (i + 1)],
+                rhs=gap[b][0][:].bitcast(FP8X4),
+                rhs_scale=gap[b][1][:],
+                start=(b == 0),
+                stop=(b == 1),
+            )
+
+        tiles = N // P
+        load_acc = [bank(i, "load%d" % i) for i in range(tiles)]
+        y_acc = [bank(tiles + i, "y%d" % i) for i in range(2)]
+        for i in range(tiles):
+            load_pass(load_acc[i], i, 0)
+        for i in range(2):
+            y_pass(y_acc[i], i, 0)
+        th = []
+        for i in range(tiles):
+            load_pass(load_acc[i], i, 1)
+            th.append(sb([P, PAIRS], F32, "th%d" % i))
+            nc.scalar.activation(th[i][:], load_acc[i][:], ACT.Tanh, bias=b3_sb[:, i : i + 1])
+        for i in range(2, tiles):
+            y_acc.append(bank(tiles + i, "y%d" % i))
+            y_pass(y_acc[i], i, 0)
+        for i in range(tiles):
+            y_pass(y_acc[i], i, 1)
+            res = sb([P, PAIRS], F32, "res%d" % i)
+            nc.vector.tensor_tensor(res[:], y_acc[i][:], th[i][:], ALU.mult)
+            nc.sync.dma_start(out[P * i : P * (i + 1), :], res[:])

@@ -46,9 +46,7 @@ def tile_list_sector_encounter_complexity_kernel(
         nc.vector.memset(tab_s[:].bitcast(I32), 0)
         warm_in = sb([P, 1], F32, "warm_in", "tab_w1")
         warm_out = sb([P, 1], F32, "warm_out", "stage_b")
-        warm_bias = sb([P, 1], F32, "warm_bias", "stage_a")
         nc.vector.memset(warm_in[:], 0.0)
-        nc.vector.memset(warm_bias[:], 0.0)
         v_scale1 = sb([P, S], U8, "v_scale1")
         nc.vector.memset(v_scale1[:].bitcast(I32), 0)
 
@@ -58,7 +56,7 @@ def tile_list_sector_encounter_complexity_kernel(
         rows = tab_scales.bitcast(I32).rearrange("a (q r) c -> r q a c", r=4)
         for r in range(4):
             nc.scalar.dma_start(tab_s[:].bitcast(I32)[r:P:16, :], rows[r])
-        nc.scalar.activation(warm_out[:], warm_in[:], ACT.Tanh, bias=warm_bias[:])
+        nc.scalar.activation(warm_out[:], warm_in[:], ACT.Tanh)
 
         def load_w1(b, a, tag):
             raw = sb([P, PACK, KP], F32, "w1raw_%d%d" % (b, a), tag)
@@ -150,10 +148,10 @@ def tile_list_sector_encounter_complexity_kernel(
             nc.vector.tensor_copy(first[:, t, :], h[b][t][:].indirect(pos1_sb[:, cols]))
             nc.vector.tensor_copy(second[:, t, :], h[b][t][:].indirect(pos2_sb[:, cols]))
 
-        def combine(op, first, second, g, parts):
+        def combine(engine, op, first, second, g, parts):
             w = PAIRS // parts
             for c0 in range(0, PAIRS, w):
-                nc.vector.tensor_tensor(
+                engine.tensor_tensor(
                     g[:, PACK * c0 : PACK * (c0 + w)].rearrange("p (c i t) -> p c t i", i=2, t=PACK),
                     first[:, :, c0 : c0 + w].rearrange("p t (c i) -> p c t i", i=2),
                     second[:, :, c0 : c0 + w].rearrange("p t (c i) -> p c t i", i=2),
@@ -165,7 +163,7 @@ def tile_list_sector_encounter_complexity_kernel(
 
         first0 = sb([P, PACK, PAIRS], F32, "first0", "first")
         second0 = sb([P, PACK, PAIRS], F32, "second0", "second")
-        for t in range(2):
+        for t in range(3):
             stage1(0, t)
             pick(0, t, first0, second0, 0, PAIRS)
         raw10 = load_w1(1, 0, "stage_b")
@@ -173,22 +171,20 @@ def tile_list_sector_encounter_complexity_kernel(
         g10 = sb([P, KP * PACK], BF16, "g10", "grp_a")
         cast_w1(raw10, g10)
         quantize_w1(g10, 1, 0, 0, [KP])
-        for t in range(2, PACK):
-            stage1(0, t)
-            pick(0, t, first0, second0, 0, PAIRS)
+        stage1(0, 3)
+        pick(0, 3, first0, second0, 0, PAIRS)
         g11 = sb([P, KP * PACK], BF16, "g11", "grp_b")
         cast_w1(raw11, g11)
         quantize_w1(g11, 1, 1, 0, [KP])
         for t in range(PACK):
             stage1(1, t)
         peak0_bf = sb([P, PAIRS * PACK], BF16, "peak0_bf", "grp_b")
-        combine(ALU.max, first0, second0, peak0_bf, 1)
-        gap_bf = sb([P, PAIRS * PACK], BF16, "gap0_bf", "gap_bf")
-        combine(ALU.subtract, first0, second0, gap_bf, 1)
-        gap = [operand("gap0")]
-        quantize(gap_bf, gap[0][0], gap[0][1], [PAIRS])
+        combine(nc.vector, ALU.max, first0, second0, peak0_bf, 2)
+        peak = [operand("peak0")]
+        quantize(peak0_bf, peak[0][0], peak[0][1], [PAIRS // 2] * 2)
+        gap0_bf = sb([P, PAIRS * PACK], BF16, "gap0_bf", "grp_b")
+        combine(nc.gpsimd, ALU.subtract, first0, second0, gap0_bf, 4)
 
-        w3_codes = [sb([P, N], U32, "w3c%d" % b) for b in range(2)]
         w3_scales = [sb([P, N], U8, "w3s%d" % b) for b in range(2)]
         w3_raw = []
         for b in range(2):
@@ -203,31 +199,35 @@ def tile_list_sector_encounter_complexity_kernel(
         rows2 = w2_scales.bitcast(I32).rearrange("a (q r) c -> r q a c", r=4)
         for r in range(4):
             nc.sync.dma_start(w2s.bitcast(I32)[r:P:32, :, :], rows2[r])
+        g3 = []
         for b in range(2):
-            g3 = sb([P, N * PACK], BF16, "g3_%d" % b)
+            g3.append(sb([P, N * PACK], BF16, "g3_%d" % b))
             for c0, w in ((0, 512), (512, 256)):
                 nc.scalar.copy(
-                    g3[:, PACK * c0 : PACK * (c0 + w)].rearrange("p (c i j) -> p c j i", i=2, j=PACK),
+                    g3[b][:, PACK * c0 : PACK * (c0 + w)].rearrange("p (c i j) -> p c j i", i=2, j=PACK),
                     w3_raw[b][:, :, c0 : c0 + w].rearrange("p j (c i) -> p c j i", i=2),
                 )
-            quantize(g3, w3_codes[b], w3_scales[b], [512, 256])
 
         b3_sb = sb([P, N // P], F32, "b3_sb", "stage_b")
         with nc.allow_non_contiguous_dma(reason="one bias value for each partition"):
             nc.sync.dma_start(b3_sb[:], b3.rearrange("(i p) -> p i", p=P))
 
-        first1 = sb([P, PACK, PAIRS], F32, "first1", "first")
-        second1 = sb([P, PACK, PAIRS], F32, "second1", "second")
+        first1 = sb([P, PACK, PAIRS], F32, "first1")
+        second1 = sb([P, PACK, PAIRS], F32, "second1")
         for t in range(PACK):
             pick(1, t, first1, second1, 0, PAIRS)
-        peak = [operand("peak0", "h13")]
-        quantize(peak0_bf, peak[0][0], peak[0][1], [PAIRS])
+        gap = [operand("gap0", "h12")]
+        quantize(gap0_bf, gap[0][0], gap[0][1], [PAIRS])
+        w3_both = sb([P, 2 * N], U32, "w3c", "h13")
+        w3_codes = [w3_both[:, N * b : N * (b + 1)] for b in range(2)]
+        for b in range(2):
+            quantize(g3[b], w3_codes[b], w3_scales[b], [512, 256])
         peak1_bf = sb([P, PAIRS * PACK], BF16, "peak1_bf")
-        combine(ALU.max, first1, second1, peak1_bf, 2)
+        combine(nc.vector, ALU.max, first1, second1, peak1_bf, 2)
         peak.append(operand("peak1"))
         quantize(peak1_bf, peak[1][0], peak[1][1], [PAIRS // 2] * 2)
         gap_bf = sb([P, PAIRS * PACK], BF16, "gap1_bf", "gap_bf")
-        combine(ALU.subtract, first1, second1, gap_bf, 2)
+        combine(nc.vector, ALU.subtract, first1, second1, gap_bf, 2)
         gap.append(operand("gap1"))
         quantize(gap_bf, gap[1][0], gap[1][1], [PAIRS // 2] * 2)
 

@@ -42,21 +42,20 @@ def tile_list_sector_encounter_complexity_kernel(
         pos1_sb = lists.tile([P, PAIRS // 16], U16, name="pos1_sb")
         pos2_sb = lists.tile([P, PAIRS // 16], U16, name="pos2_sb")
 
-        tab_s = sb([P, T], U8, "tab_s")
-        nc.vector.memset(tab_s[:].bitcast(I32), 0)
-        warm_in = sb([P, 1], F32, "warm_in", "tab_w1")
-        warm_out = sb([P, 1], F32, "warm_out", "stage_b")
-        nc.vector.memset(warm_in[:], 0.0)
-        v_scale1 = sb([P, S], U8, "v_scale1")
-        nc.vector.memset(v_scale1[:].bitcast(I32), 0)
-
         nc.sync.dma_start(offs_sb[:], offs)
-        tab_w = [sb([P, T], U16, "tab_w0")]
-        nc.sync.dma_start(tab_w[0][:].bitcast(I32), tab_words[0].bitcast(I32))
-        rows = tab_scales.bitcast(I32).rearrange("a (q r) c -> r q a c", r=4)
-        for r in range(4):
-            nc.scalar.dma_start(tab_s[:].bitcast(I32)[r:P:16, :], rows[r])
+        tab_s = sb([P, T], U8, "tab_s")
+        nc.sync.dma_start(tab_s[:].bitcast(I32)[0:32, :], tab_scales.bitcast(I32).rearrange("a q c -> (a q) c"))
+        nc.vector.memset(tab_s[:].bitcast(I32)[32:64, :], 0)
+        nc.vector.memset(tab_s[:].bitcast(I32)[64:P, :], 0)
+        warm_in = sb([P, 1], F32, "warm_in")
+        warm_out = sb([P, 1], F32, "warm_out")
+        nc.vector.memset(warm_in[:], 0.0)
         nc.scalar.activation(warm_out[:], warm_in[:], ACT.Tanh)
+        v_scales = [sb([P, S], U8, "v_scale%d" % a) for a in range(2)]
+        for a in range(2):
+            nc.vector.memset(v_scales[a][:].bitcast(I32), 0)
+        tab_w = [sb([P, T], U16, "tab_w%d" % a) for a in range(2)]
+        nc.sync.dma_start(tab_w[0][:].bitcast(I32), tab_words[0].bitcast(I32))
 
         def load_w1(b, a, tag):
             raw = sb([P, PACK, KP], F32, "w1raw_%d%d" % (b, a), tag)
@@ -81,20 +80,27 @@ def tile_list_sector_encounter_complexity_kernel(
                 c = c + w
 
         raw00 = load_w1(0, 0, "stage_a")
-        tab_w.append(sb([P, T], U16, "tab_w1"))
         nc.sync.dma_start(tab_w[1][:].bitcast(I32), tab_words[1].bitcast(I32))
-        raw01 = load_w1(0, 1, "stage_b")
         nc.sync.dma_start(pos1_sb[:], pos1)
         nc.sync.dma_start(pos2_sb[:], pos2)
 
         v_words = [sb([P, S], U16, "v_words%d" % a) for a in range(2)]
-        v_scale0 = sb([P, S], U8, "v_scale0")
-        nc.vector.tensor_copy(v_words[0][:], tab_w[0][:].indirect(offs_sb[:]))
-        nc.vector.tensor_copy(v_scale0[:], tab_s[:].indirect(offs_sb[:]))
-        nc.vector.tensor_copy(v_words[1][:], tab_w[1][:].indirect(offs_sb[:]))
-        nc.sync.dma_start(v_scale1[:].bitcast(I32)[0 : P - 16, :], v_scale0[:].bitcast(I32)[16:P, :])
-        v_scales = [v_scale0, v_scale1]
-        b1_sb = sb([P, 2, PACK], F32, "b1_sb", "tab_s")
+        v_rows = sb([P, S], U8, "v_rows")
+        nc.vector.tensor_copy(v_rows[:], tab_s[:].indirect(offs_sb[:]))
+        for a in range(2):
+            nc.vector.tensor_copy(v_words[a][:], tab_w[a][:].indirect(offs_sb[:]))
+
+        def place_scales(a):
+            for q in range(4):
+                r0 = 16 * a + 4 * q
+                nc.sync.dma_start(
+                    v_scales[a][:].bitcast(I32)[32 * q : 32 * q + 4, :], v_rows[:].bitcast(I32)[r0 : r0 + 4, :]
+                )
+
+        place_scales(0)
+        raw01 = load_w1(0, 1, "tab_s")
+        place_scales(1)
+        b1_sb = sb([P, 2, PACK], F32, "b1_sb", "tab_w0")
         nc.sync.dma_start(b1_sb[:], b1.rearrange("(b p t) -> p b t", p=P, t=PACK))
 
         w1_q = {}
@@ -110,16 +116,14 @@ def tile_list_sector_encounter_complexity_kernel(
 
         h = [[sb([P, S], F32, "h%d%d" % (b, t)) for t in range(PACK)] for b in range(2)]
 
-        g00 = sb([P, KP * PACK], BF16, "g00", "grp_a")
-        cast_w1(raw00, g00)
-        quantize_w1(g00, 0, 0, 0, [KP])
-        for u, copy in enumerate((nc.vector.tensor_copy, nc.scalar.copy)):
-            g01 = sb([P, KP * 2], BF16, "g01_%d" % u, ("grp_b", "grp_c")[u])
-            copy(
-                g01[:].rearrange("p (e q j) -> p q j e", e=2, j=PACK),
-                raw01[:].rearrange("p j (q u e) -> p u q j e", u=2, e=2)[:, u],
-            )
-            quantize_w1(g01, 0, 1, 2 * u, [P, P] if u == 0 else [2 * P])
+        for a, raw in enumerate((raw00, raw01)):
+            for u, copy in enumerate((nc.vector.tensor_copy, nc.scalar.copy)):
+                g = sb([P, KP * 2], BF16, "g0%d_%d" % (a, u), (("grp_a", "grp_d"), ("grp_b", "grp_c"))[a][u])
+                copy(
+                    g[:].rearrange("p (e q j) -> p q j e", e=2, j=PACK),
+                    raw[:].rearrange("p j (q u e) -> p u q j e", u=2, e=2)[:, u],
+                )
+                quantize_w1(g, 0, a, 2 * u, [P, P] if (a, u) == (1, 0) else [2 * P])
 
         def stage1(b, t):
             banks = [bank(4 * b + (2 * t + m) % 4, "acc%d%d%d" % (b, t, m)) for m in range(2)]
@@ -166,7 +170,7 @@ def tile_list_sector_encounter_complexity_kernel(
         for t in range(3):
             stage1(0, t)
             pick(0, t, first0, second0, 0, PAIRS)
-        raw10 = load_w1(1, 0, "stage_b")
+        raw10 = load_w1(1, 0, "tab_s")
         raw11 = load_w1(1, 1, "grp_c")
         g10 = sb([P, KP * PACK], BF16, "g10", "grp_a")
         cast_w1(raw10, g10)
@@ -179,16 +183,16 @@ def tile_list_sector_encounter_complexity_kernel(
         for t in range(PACK):
             stage1(1, t)
         peak0_bf = sb([P, PAIRS * PACK], BF16, "peak0_bf", "grp_b")
-        combine(nc.vector, ALU.max, first0, second0, peak0_bf, 2)
+        combine(nc.vector, ALU.max, first0, second0, peak0_bf, 1)
+        gap0_bf = sb([P, PAIRS * PACK], BF16, "gap0_bf", "gap_bf")
+        combine(nc.vector, ALU.subtract, first0, second0, gap0_bf, 1)
         peak = [operand("peak0")]
-        quantize(peak0_bf, peak[0][0], peak[0][1], [PAIRS // 2] * 2)
-        gap0_bf = sb([P, PAIRS * PACK], BF16, "gap0_bf", "grp_b")
-        combine(nc.gpsimd, ALU.subtract, first0, second0, gap0_bf, 4)
+        quantize(peak0_bf, peak[0][0], peak[0][1], [PAIRS])
 
         w3_scales = [sb([P, N], U8, "w3s%d" % b) for b in range(2)]
         w3_raw = []
         for b in range(2):
-            raw = sb([P, PACK, N], F32, "w3raw%d" % b, ("stage_b", "grp_c")[b])
+            raw = sb([P, PACK, N], F32, "w3raw%d" % b, ("tab_s", "grp_c")[b])
             nc.sync.dma_start(raw[:], w3[KP * b : KP * (b + 1), :].rearrange("(p j) c -> p j c", j=PACK))
             w3_raw.append(raw)
         w2 = sb([P, 6 * N], U8, "w2", "grp_a")
@@ -208,25 +212,27 @@ def tile_list_sector_encounter_complexity_kernel(
                     w3_raw[b][:, :, c0 : c0 + w].rearrange("p j (c i) -> p c j i", i=2),
                 )
 
-        b3_sb = sb([P, N // P], F32, "b3_sb", "stage_b")
+        b3_sb = sb([P, N // P], F32, "b3_sb", "tab_s")
         with nc.allow_non_contiguous_dma(reason="one bias value for each partition"):
             nc.sync.dma_start(b3_sb[:], b3.rearrange("(i p) -> p i", p=P))
 
-        first1 = sb([P, PACK, PAIRS], F32, "first1")
-        second1 = sb([P, PACK, PAIRS], F32, "second1")
-        for t in range(PACK):
+        first1 = sb([P, PACK, PAIRS], F32, "first1", "first")
+        second1 = sb([P, PACK, PAIRS], F32, "second1", "second")
+        for t in range(PACK - 1):
             pick(1, t, first1, second1, 0, PAIRS)
-        gap = [operand("gap0", "h12")]
+        w3_codes = [sb([P, N], U32, "w3c0", "h12")]
+        quantize(g3[0], w3_codes[0], w3_scales[0], [512, 256])
+        pick(1, PACK - 1, first1, second1, 0, PAIRS)
+        late = sb([P, N + PAIRS], U32, "late", "h13")
+        w3_codes.append(late[:, :N])
+        quantize(g3[1], w3_codes[1], w3_scales[1], [512, 256])
+        gap = [(late[:, N:], sb([P, PAIRS], U8, "gap0_s"))]
         quantize(gap0_bf, gap[0][0], gap[0][1], [PAIRS])
-        w3_both = sb([P, 2 * N], U32, "w3c", "h13")
-        w3_codes = [w3_both[:, N * b : N * (b + 1)] for b in range(2)]
-        for b in range(2):
-            quantize(g3[b], w3_codes[b], w3_scales[b], [512, 256])
         peak1_bf = sb([P, PAIRS * PACK], BF16, "peak1_bf")
         combine(nc.vector, ALU.max, first1, second1, peak1_bf, 2)
         peak.append(operand("peak1"))
         quantize(peak1_bf, peak[1][0], peak[1][1], [PAIRS // 2] * 2)
-        gap_bf = sb([P, PAIRS * PACK], BF16, "gap1_bf", "gap_bf")
+        gap_bf = sb([P, PAIRS * PACK], BF16, "gap1_bf")
         combine(nc.vector, ALU.subtract, first1, second1, gap_bf, 2)
         gap.append(operand("gap1"))
         quantize(gap_bf, gap[1][0], gap[1][1], [PAIRS // 2] * 2)
@@ -265,10 +271,10 @@ def tile_list_sector_encounter_complexity_kernel(
             load_pass(load_acc[i], i, 1)
             th.append(sb([P, PAIRS], F32, "th%d" % i))
             nc.scalar.activation(th[i][:], load_acc[i][:], ACT.Tanh, bias=b3_sb[:, i : i + 1])
-        for i in range(2, tiles):
-            y_acc.append(bank(tiles + i, "y%d" % i))
-            y_pass(y_acc[i], i, 0)
         for i in range(tiles):
+            if i >= 2:
+                y_acc.append(bank(tiles + i, "y%d" % i))
+                y_pass(y_acc[i], i, 0)
             y_pass(y_acc[i], i, 1)
             res = sb([P, PAIRS], F32, "res%d" % i)
             nc.vector.tensor_tensor(res[:], y_acc[i][:], th[i][:], ALU.mult)

@@ -19,8 +19,13 @@ ALU = mybir.AluOpType
 P = 128
 PACK = 4
 KP = P * PACK
+QUAD = 32
 BANK = 512
-AL = 64
+BANKS = 8
+ALIGN = 64
+W3_PARTS = (512, 256)
+GPSIMD_PARTS = 4
+EARLY_Y = BANKS - N // P
 
 
 def tile_list_sector_encounter_complexity_kernel(
@@ -33,41 +38,10 @@ def tile_list_sector_encounter_complexity_kernel(
         psum = ctx.enter_context(tc.psum_pool(name="psum", bufs=1))
 
         def sb(shape, dtype, name, tag=None):
-            return keep.tile(shape, dtype, name=name, tag=tag or name, align_bytes=AL)
+            return keep.tile(shape, dtype, name=name, tag=tag or name, align_bytes=ALIGN)
 
         def bank(i, name):
-            return psum.tile([P, BANK], F32, name=name, tag="bank%d" % (i % 8))
-
-        offs_sb = lists.tile([P, S // 16], U16, name="offs_sb")
-        pos1_sb = lists.tile([P, PAIRS // 16], U16, name="pos1_sb")
-        pos2_sb = lists.tile([P, PAIRS // 16], U16, name="pos2_sb")
-
-        nc.sync.dma_start(offs_sb[:], offs)
-        tab_s = sb([P, T], U8, "tab_s")
-        nc.sync.dma_start(tab_s[:].bitcast(I32)[0:32, :], tab_scales.bitcast(I32).rearrange("a q c -> (a q) c"))
-        nc.vector.memset(tab_s[:].bitcast(I32)[32:64, :], 0)
-        nc.vector.memset(tab_s[:].bitcast(I32)[64:P, :], 0)
-        warm_in = sb([P, 1], F32, "warm_in")
-        warm_out = sb([P, 1], F32, "warm_out")
-        nc.vector.memset(warm_in[:], 0.0)
-        nc.scalar.activation(warm_out[:], warm_in[:], ACT.Tanh)
-        v_scales = [sb([P, S], U8, "v_scale%d" % a) for a in range(2)]
-        for a in range(2):
-            nc.vector.memset(v_scales[a][:].bitcast(I32), 0)
-        tab_w = [sb([P, T], U16, "tab_w%d" % a) for a in range(2)]
-        nc.sync.dma_start(tab_w[0][:].bitcast(I32), tab_words[0].bitcast(I32))
-
-        def load_w1(b, a, tag):
-            raw = sb([P, PACK, KP], F32, "w1raw_%d%d" % (b, a), tag)
-            src = w1[KP * a : KP * (a + 1), KP * b : KP * (b + 1)]
-            nc.sync.dma_start(raw[:], src.rearrange("(p j) c -> p j c", j=PACK))
-            return raw
-
-        def cast_w1(raw, grouped):
-            nc.scalar.copy(
-                grouped[:].rearrange("p (u e q j) -> p q u j e", u=2, e=2, j=PACK),
-                raw[:].rearrange("p j (q u e) -> p q u j e", u=2, e=2),
-            )
+            return psum.tile([P, BANK], F32, name=name, tag="bank%d" % (i % BANKS))
 
         def quantize(grouped, codes, scales, widths):
             c = 0
@@ -79,7 +53,27 @@ def tile_list_sector_encounter_complexity_kernel(
                 )
                 c = c + w
 
-        raw00 = load_w1(0, 0, "stage_a")
+        def load_w1(b, a, tag):
+            raw = sb([P, PACK, KP], F32, "w1raw_%d%d" % (b, a), tag)
+            src = w1[KP * a : KP * (a + 1), KP * b : KP * (b + 1)]
+            nc.sync.dma_start(raw[:], src.rearrange("(p j) c -> p j c", j=PACK))
+            return raw
+
+        offs_sb = lists.tile([P, S // 16], U16, name="offs_sb")
+        pos1_sb = lists.tile([P, PAIRS // 16], U16, name="pos1_sb")
+        pos2_sb = lists.tile([P, PAIRS // 16], U16, name="pos2_sb")
+
+        nc.sync.dma_start(offs_sb[:], offs)
+        tab_s = sb([P, T], U8, "tab_s")
+        nc.sync.dma_start(tab_s[:].bitcast(I32)[0:QUAD, :], tab_scales.bitcast(I32).rearrange("a g c -> (a g) c"))
+        nc.vector.memset(tab_s[:].bitcast(I32)[QUAD : 2 * QUAD, :], 0)
+        nc.vector.memset(tab_s[:].bitcast(I32)[2 * QUAD : P, :], 0)
+        v_scales = [sb([P, S], U8, "v_scale%d" % a) for a in range(2)]
+        for a in range(2):
+            nc.vector.memset(v_scales[a][:].bitcast(I32), 0)
+        tab_w = [sb([P, T], U16, "tab_w%d" % a) for a in range(2)]
+        nc.sync.dma_start(tab_w[0][:].bitcast(I32), tab_words[0].bitcast(I32))
+        raw00 = load_w1(0, 0, "w1raw_first")
         nc.sync.dma_start(tab_w[1][:].bitcast(I32), tab_words[1].bitcast(I32))
         nc.sync.dma_start(pos1_sb[:], pos1)
         nc.sync.dma_start(pos2_sb[:], pos2)
@@ -91,10 +85,11 @@ def tile_list_sector_encounter_complexity_kernel(
             nc.vector.tensor_copy(v_words[a][:], tab_w[a][:].indirect(offs_sb[:]))
 
         def place_scales(a):
-            for q in range(4):
-                r0 = 16 * a + 4 * q
+            for q in range(P // QUAD):
+                r0 = 16 * a + PACK * q
                 nc.sync.dma_start(
-                    v_scales[a][:].bitcast(I32)[32 * q : 32 * q + 4, :], v_rows[:].bitcast(I32)[r0 : r0 + 4, :]
+                    v_scales[a][:].bitcast(I32)[QUAD * q : QUAD * q + PACK, :],
+                    v_rows[:].bitcast(I32)[r0 : r0 + PACK, :],
                 )
 
         place_scales(0)
@@ -105,30 +100,36 @@ def tile_list_sector_encounter_complexity_kernel(
 
         w1_q = {}
 
-        def quantize_w1(grouped, b, a, t0, widths, tag=None):
+        def quantize_w1(grouped, b, a, t0, widths):
             n = sum(widths)
-            codes = sb([P, n], U32, "w1c%d%d%d" % (b, a, t0), tag)
+            codes = sb([P, n], U32, "w1c%d%d%d" % (b, a, t0))
             scales = sb([P, n], U8, "w1s%d%d%d" % (b, a, t0))
             quantize(grouped, codes, scales, widths)
             for t in range(t0, t0 + n // P):
                 cols = slice(P * (t - t0), P * (t - t0 + 1))
                 w1_q[b, a, t] = (codes[:, cols].bitcast(FP8X4), scales[:, cols])
 
+        def cast_w1(raw, grouped):
+            nc.scalar.copy(
+                grouped[:].rearrange("p (u e q j) -> p q u j e", u=2, e=2, j=PACK),
+                raw[:].rearrange("p j (q u e) -> p q u j e", u=2, e=2),
+            )
+
         h = [[sb([P, S], F32, "h%d%d" % (b, t)) for t in range(PACK)] for b in range(2)]
 
         for a, raw in enumerate((raw00, raw01)):
             for u, copy in enumerate((nc.vector.tensor_copy, nc.scalar.copy)):
-                g = sb([P, KP * 2], BF16, "g0%d_%d" % (a, u), (("grp_a", "grp_d"), ("grp_b", "grp_c"))[a][u])
+                half = sb([P, KP * 2], BF16, "w1bf_0%d_%d" % (a, u), (("bf_a", "bf_d"), ("bf_b", "bf_c"))[a][u])
                 copy(
-                    g[:].rearrange("p (e q j) -> p q j e", e=2, j=PACK),
+                    half[:].rearrange("p (e q j) -> p q j e", e=2, j=PACK),
                     raw[:].rearrange("p j (q u e) -> p u q j e", u=2, e=2)[:, u],
                 )
-                quantize_w1(g, 0, a, 2 * u, [P, P] if (a, u) == (1, 0) else [2 * P])
+                quantize_w1(half, 0, a, 2 * u, [P, P] if (a, u) == (1, 0) else [2 * P])
 
         def stage1(b, t):
-            banks = [bank(4 * b + (2 * t + m) % 4, "acc%d%d%d" % (b, t, m)) for m in range(2)]
+            banks = [bank(4 * b + (2 * t + m) % 4, "acc%d%d%d" % (b, t, m)) for m in range(S // BANK)]
             for a in range(2):
-                for m in range(2):
+                for m in range(S // BANK):
                     cols = slice(BANK * m, BANK * (m + 1))
                     nc.tensor.matmul_mx(
                         out=banks[m][:],
@@ -139,7 +140,7 @@ def tile_list_sector_encounter_complexity_kernel(
                         start=(a == 0),
                         stop=(a == 1),
                     )
-            for m in range(2):
+            for m in range(S // BANK):
                 cols = slice(BANK * m, BANK * (m + 1))
                 bias = b1_sb[:, b, t : t + 1]
                 if (b, t, m) == (0, 0, 1):
@@ -147,95 +148,92 @@ def tile_list_sector_encounter_complexity_kernel(
                 else:
                     nc.scalar.activation(h[b][t][:, cols], banks[m][:], ACT.Identity, bias=bias)
 
-        def pick(b, t, first, second, j0, w):
-            cols = slice(j0 // 16, (j0 + w) // 16)
-            nc.vector.tensor_copy(first[:, t, :], h[b][t][:].indirect(pos1_sb[:, cols]))
-            nc.vector.tensor_copy(second[:, t, :], h[b][t][:].indirect(pos2_sb[:, cols]))
+        def pick(b, t, first, second):
+            nc.vector.tensor_copy(first[:, t, :], h[b][t][:].indirect(pos1_sb[:]))
+            nc.vector.tensor_copy(second[:, t, :], h[b][t][:].indirect(pos2_sb[:]))
 
-        def combine(engine, op, first, second, g, parts):
+        def combine(engine, op, first, second, grouped, parts):
             w = PAIRS // parts
             for c0 in range(0, PAIRS, w):
                 engine.tensor_tensor(
-                    g[:, PACK * c0 : PACK * (c0 + w)].rearrange("p (c i t) -> p c t i", i=2, t=PACK),
+                    grouped[:, PACK * c0 : PACK * (c0 + w)].rearrange("p (c i t) -> p c t i", i=2, t=PACK),
                     first[:, :, c0 : c0 + w].rearrange("p t (c i) -> p c t i", i=2),
                     second[:, :, c0 : c0 + w].rearrange("p t (c i) -> p c t i", i=2),
                     op,
                 )
 
-        def operand(name, tag=None):
-            return sb([P, PAIRS], U32, name + "_c", tag), sb([P, PAIRS], U8, name + "_s")
+        def operand(name):
+            return sb([P, PAIRS], U32, name + "_c"), sb([P, PAIRS], U8, name + "_s")
 
-        first0 = sb([P, PACK, PAIRS], F32, "first0", "first")
-        second0 = sb([P, PACK, PAIRS], F32, "second0", "second")
-        for t in range(3):
+        first0 = sb([P, PACK, PAIRS], F32, "first0")
+        second0 = sb([P, PACK, PAIRS], F32, "second0")
+        for t in range(PACK - 1):
             stage1(0, t)
-            pick(0, t, first0, second0, 0, PAIRS)
+            pick(0, t, first0, second0)
         raw10 = load_w1(1, 0, "tab_s")
-        raw11 = load_w1(1, 1, "grp_c")
-        g10 = sb([P, KP * PACK], BF16, "g10", "grp_a")
-        cast_w1(raw10, g10)
-        quantize_w1(g10, 1, 0, 0, [KP])
-        stage1(0, 3)
-        pick(0, 3, first0, second0, 0, PAIRS)
-        g11 = sb([P, KP * PACK], BF16, "g11", "grp_b")
-        cast_w1(raw11, g11)
-        quantize_w1(g11, 1, 1, 0, [KP])
+        raw11 = load_w1(1, 1, "bf_c")
+        w1bf_10 = sb([P, KP * PACK], BF16, "w1bf_10", "bf_a")
+        cast_w1(raw10, w1bf_10)
+        quantize_w1(w1bf_10, 1, 0, 0, [KP])
+        stage1(0, PACK - 1)
+        pick(0, PACK - 1, first0, second0)
+        w1bf_11 = sb([P, KP * PACK], BF16, "w1bf_11", "bf_b")
+        cast_w1(raw11, w1bf_11)
+        quantize_w1(w1bf_11, 1, 1, 0, [KP])
         for t in range(PACK):
             stage1(1, t)
-        peak0_bf = sb([P, PAIRS * PACK], BF16, "peak0_bf", "grp_b")
-        combine(nc.vector, ALU.max, first0, second0, peak0_bf, 1)
-        gap0_bf = sb([P, PAIRS * PACK], BF16, "gap0_bf", "gap_bf")
-        combine(nc.vector, ALU.subtract, first0, second0, gap0_bf, 1)
+
+        peak0_bf = sb([P, PAIRS * PACK], BF16, "peak0_bf", "bf_b")
+        combine(nc.vector, ALU.max, first0, second0, peak0_bf, 2)
         peak = [operand("peak0")]
-        quantize(peak0_bf, peak[0][0], peak[0][1], [PAIRS])
+        quantize(peak0_bf, peak[0][0], peak[0][1], [PAIRS // 2] * 2)
+        gap0_bf = sb([P, PAIRS * PACK], BF16, "gap0_bf", "bf_b")
+        combine(nc.gpsimd, ALU.subtract, first0, second0, gap0_bf, GPSIMD_PARTS)
 
         w3_scales = [sb([P, N], U8, "w3s%d" % b) for b in range(2)]
         w3_raw = []
         for b in range(2):
-            raw = sb([P, PACK, N], F32, "w3raw%d" % b, ("tab_s", "grp_c")[b])
+            raw = sb([P, PACK, N], F32, "w3raw%d" % b, ("tab_s", "bf_c")[b])
             nc.sync.dma_start(raw[:], w3[KP * b : KP * (b + 1), :].rearrange("(p j) c -> p j c", j=PACK))
             w3_raw.append(raw)
-        w2 = sb([P, 6 * N], U8, "w2", "grp_a")
-        w2w = w2[:, : 4 * N].rearrange("p (a c) -> p a c", a=2)
-        w2s = w2[:, 4 * N :].rearrange("p (a c) -> p a c", a=2)
-        nc.sync.dma_start(w2w.bitcast(I32), w2_words.bitcast(I32).rearrange("a p c -> p a c"))
+        w2 = sb([P, 6 * N], U8, "w2", "bf_a")
+        w2w = w2[:, : 4 * N].rearrange("p (b c) -> p b c", b=2)
+        w2s = w2[:, 4 * N :].rearrange("p (b c) -> p b c", b=2)
+        nc.sync.dma_start(w2w.bitcast(I32), w2_words.bitcast(I32).rearrange("b p c -> p b c"))
         nc.gpsimd.memset(w2[:, 4 * N :].bitcast(I32), 0)
-        rows2 = w2_scales.bitcast(I32).rearrange("a (q r) c -> r q a c", r=4)
-        for r in range(4):
-            nc.sync.dma_start(w2s.bitcast(I32)[r:P:32, :, :], rows2[r])
-        g3 = []
+        w2_rows = w2_scales.bitcast(I32).rearrange("b (q r) c -> r q b c", r=PACK)
+        for r in range(PACK):
+            nc.sync.dma_start(w2s.bitcast(I32)[r:P:QUAD, :, :], w2_rows[r])
+        w3_bf = []
         for b in range(2):
-            g3.append(sb([P, N * PACK], BF16, "g3_%d" % b))
-            for c0, w in ((0, 512), (512, 256)):
+            w3_bf.append(sb([P, N * PACK], BF16, "w3bf_%d" % b))
+            for c0, w in ((0, W3_PARTS[0]), (W3_PARTS[0], W3_PARTS[1])):
                 nc.scalar.copy(
-                    g3[b][:, PACK * c0 : PACK * (c0 + w)].rearrange("p (c i j) -> p c j i", i=2, j=PACK),
+                    w3_bf[b][:, PACK * c0 : PACK * (c0 + w)].rearrange("p (c i j) -> p c j i", i=2, j=PACK),
                     w3_raw[b][:, :, c0 : c0 + w].rearrange("p j (c i) -> p c j i", i=2),
                 )
-
         b3_sb = sb([P, N // P], F32, "b3_sb", "tab_s")
         with nc.allow_non_contiguous_dma(reason="one bias value for each partition"):
             nc.sync.dma_start(b3_sb[:], b3.rearrange("(i p) -> p i", p=P))
 
-        first1 = sb([P, PACK, PAIRS], F32, "first1", "first")
-        second1 = sb([P, PACK, PAIRS], F32, "second1", "second")
-        for t in range(PACK - 1):
-            pick(1, t, first1, second1, 0, PAIRS)
-        w3_codes = [sb([P, N], U32, "w3c0", "h12")]
-        quantize(g3[0], w3_codes[0], w3_scales[0], [512, 256])
-        pick(1, PACK - 1, first1, second1, 0, PAIRS)
-        late = sb([P, N + PAIRS], U32, "late", "h13")
-        w3_codes.append(late[:, :N])
-        quantize(g3[1], w3_codes[1], w3_scales[1], [512, 256])
-        gap = [(late[:, N:], sb([P, PAIRS], U8, "gap0_s"))]
+        first1 = sb([P, PACK, PAIRS], F32, "first1")
+        second1 = sb([P, PACK, PAIRS], F32, "second1")
+        for t in range(PACK):
+            pick(1, t, first1, second1)
+        late_codes = sb([P, 2 * N + PAIRS], U32, "late_codes", "h13")
+        w3_codes = [late_codes[:, N * b : N * (b + 1)] for b in range(2)]
+        for b in range(2):
+            quantize(w3_bf[b], w3_codes[b], w3_scales[b], W3_PARTS)
+        gap = [(late_codes[:, 2 * N :], sb([P, PAIRS], U8, "gap0_s"))]
         quantize(gap0_bf, gap[0][0], gap[0][1], [PAIRS])
         peak1_bf = sb([P, PAIRS * PACK], BF16, "peak1_bf")
         combine(nc.vector, ALU.max, first1, second1, peak1_bf, 2)
         peak.append(operand("peak1"))
         quantize(peak1_bf, peak[1][0], peak[1][1], [PAIRS // 2] * 2)
-        gap_bf = sb([P, PAIRS * PACK], BF16, "gap1_bf")
-        combine(nc.vector, ALU.subtract, first1, second1, gap_bf, 2)
+        gap1_bf = sb([P, PAIRS * PACK], BF16, "gap1_bf")
+        combine(nc.vector, ALU.subtract, first1, second1, gap1_bf, 2)
         gap.append(operand("gap1"))
-        quantize(gap_bf, gap[1][0], gap[1][1], [PAIRS // 2] * 2)
+        quantize(gap1_bf, gap[1][0], gap[1][1], [PAIRS // 2] * 2)
 
         def load_pass(acc, i, b):
             nc.tensor.matmul_mx(
@@ -261,21 +259,21 @@ def tile_list_sector_encounter_complexity_kernel(
 
         tiles = N // P
         load_acc = [bank(i, "load%d" % i) for i in range(tiles)]
-        y_acc = [bank(tiles + i, "y%d" % i) for i in range(2)]
+        y_acc = [bank(tiles + i, "y%d" % i) for i in range(EARLY_Y)]
         for i in range(tiles):
             load_pass(load_acc[i], i, 0)
-        for i in range(2):
+        for i in range(EARLY_Y):
             y_pass(y_acc[i], i, 0)
-        th = []
+        weight = []
         for i in range(tiles):
             load_pass(load_acc[i], i, 1)
-            th.append(sb([P, PAIRS], F32, "th%d" % i))
-            nc.scalar.activation(th[i][:], load_acc[i][:], ACT.Tanh, bias=b3_sb[:, i : i + 1])
+            weight.append(sb([P, PAIRS], F32, "weight%d" % i))
+            nc.scalar.activation(weight[i][:], load_acc[i][:], ACT.Tanh, bias=b3_sb[:, i : i + 1])
         for i in range(tiles):
-            if i >= 2:
+            if i >= EARLY_Y:
                 y_acc.append(bank(tiles + i, "y%d" % i))
                 y_pass(y_acc[i], i, 0)
             y_pass(y_acc[i], i, 1)
             res = sb([P, PAIRS], F32, "res%d" % i)
-            nc.vector.tensor_tensor(res[:], y_acc[i][:], th[i][:], ALU.mult)
+            nc.vector.tensor_tensor(res[:], y_acc[i][:], weight[i][:], ALU.mult)
             nc.sync.dma_start(out[P * i : P * (i + 1), :], res[:])

from contextlib import ExitStack

import concourse.mybir as mybir

K, T, S, H, PAIRS, N = 1024, 4096, 1024, 1024, 512, 768
FLOPS = 2 * K * H * S + 2 * 2 * H * N * PAIRS

F32 = mybir.dt.float32
BF16 = mybir.dt.bfloat16
I32 = mybir.dt.int32
U32 = mybir.dt.uint32
U16 = mybir.dt.uint16
U8 = mybir.dt.uint8
FP8X4 = mybir.dt.float8_e4m3fn_x4
FP4X4 = mybir.dt.float4_e2m1fn_x4
ACT = mybir.ActivationFunctionType
ALU = mybir.AluOpType

P = 128
PACK = 4
KP = P * PACK
QUAD = 32
BANK = 512
BANKS = 8
ALIGN = 64
W3_PARTS = (512, 256)
GPSIMD_PARTS = 4
EARLY_Y = BANKS - N // P


def tile_list_sector_encounter_complexity_kernel(
    tc, tab_words, tab_scales, offs, pos1, pos2, w1, b1, w2_words, w2_scales, w3, b3, out
):
    nc = tc.nc
    with ExitStack() as ctx:
        lists = ctx.enter_context(tc.tile_pool(name="lists", bufs=1))
        keep = ctx.enter_context(tc.tile_pool(name="keep", bufs=1))
        psum = ctx.enter_context(tc.psum_pool(name="psum", bufs=1))

        def sb(shape, dtype, name, tag=None):
            return keep.tile(shape, dtype, name=name, tag=tag or name, align_bytes=ALIGN)

        def bank(i, name):
            return psum.tile([P, BANK], F32, name=name, tag="bank%d" % (i % BANKS))

        def quantize(grouped, codes, scales, widths):
            c = 0
            for w in widths:
                nc.vector.quantize_mx(
                    out=codes[:, c : c + w].bitcast(FP8X4),
                    scales=scales[:, c : c + w],
                    in_=grouped[:, PACK * c : PACK * (c + w)],
                )
                c = c + w

        def load_w1(b, a, tag):
            raw = sb([P, PACK, KP], F32, "w1raw_%d%d" % (b, a), tag)
            src = w1[KP * a : KP * (a + 1), KP * b : KP * (b + 1)]
            nc.sync.dma_start(raw[:], src.rearrange("(p j) c -> p j c", j=PACK))
            return raw

        offs_sb = lists.tile([P, S // 16], U16, name="offs_sb")
        pos1_sb = lists.tile([P, PAIRS // 16], U16, name="pos1_sb")
        pos2_sb = lists.tile([P, PAIRS // 16], U16, name="pos2_sb")

        nc.sync.dma_start(offs_sb[:], offs)
        tab_s = sb([P, T], U8, "tab_s")
        nc.sync.dma_start(tab_s[:].bitcast(I32)[0:QUAD, :], tab_scales.bitcast(I32).rearrange("a g c -> (a g) c"))
        nc.vector.memset(tab_s[:].bitcast(I32)[QUAD : 2 * QUAD, :], 0)
        nc.vector.memset(tab_s[:].bitcast(I32)[2 * QUAD : P, :], 0)
        v_scales = [sb([P, S], U8, "v_scale%d" % a) for a in range(2)]
        for a in range(2):
            nc.vector.memset(v_scales[a][:].bitcast(I32), 0)
        tab_w = [sb([P, T], U16, "tab_w%d" % a) for a in range(2)]
        nc.sync.dma_start(tab_w[0][:].bitcast(I32), tab_words[0].bitcast(I32))
        raw00 = load_w1(0, 0, "w1raw_first")
        nc.sync.dma_start(tab_w[1][:].bitcast(I32), tab_words[1].bitcast(I32))
        nc.sync.dma_start(pos1_sb[:], pos1)
        nc.sync.dma_start(pos2_sb[:], pos2)

        v_words = [sb([P, S], U16, "v_words%d" % a) for a in range(2)]
        v_rows = sb([P, S], U8, "v_rows")
        nc.vector.tensor_copy(v_rows[:], tab_s[:].indirect(offs_sb[:]))
        for a in range(2):
            nc.vector.tensor_copy(v_words[a][:], tab_w[a][:].indirect(offs_sb[:]))

        def place_scales(a):
            for q in range(P // QUAD):
                r0 = 16 * a + PACK * q
                nc.sync.dma_start(
                    v_scales[a][:].bitcast(I32)[QUAD * q : QUAD * q + PACK, :],
                    v_rows[:].bitcast(I32)[r0 : r0 + PACK, :],
                )

        place_scales(0)
        raw01 = load_w1(0, 1, "tab_s")
        place_scales(1)
        b1_sb = sb([P, 2, PACK], F32, "b1_sb", "tab_w0")
        nc.sync.dma_start(b1_sb[:], b1.rearrange("(b p t) -> p b t", p=P, t=PACK))

        w1_q = {}

        def quantize_w1(grouped, b, a, t0, widths):
            n = sum(widths)
            codes = sb([P, n], U32, "w1c%d%d%d" % (b, a, t0))
            scales = sb([P, n], U8, "w1s%d%d%d" % (b, a, t0))
            quantize(grouped, codes, scales, widths)
            for t in range(t0, t0 + n // P):
                cols = slice(P * (t - t0), P * (t - t0 + 1))
                w1_q[b, a, t] = (codes[:, cols].bitcast(FP8X4), scales[:, cols])

        def cast_w1(raw, grouped):
            nc.scalar.copy(
                grouped[:].rearrange("p (u e q j) -> p q u j e", u=2, e=2, j=PACK),
                raw[:].rearrange("p j (q u e) -> p q u j e", u=2, e=2),
            )

        h = [[sb([P, S], F32, "h%d%d" % (b, t)) for t in range(PACK)] for b in range(2)]

        for a, raw in enumerate((raw00, raw01)):
            for u, copy in enumerate((nc.vector.tensor_copy, nc.scalar.copy)):
                half = sb([P, KP * 2], BF16, "w1bf_0%d_%d" % (a, u), (("bf_a", "bf_d"), ("bf_b", "bf_c"))[a][u])
                copy(
                    half[:].rearrange("p (e q j) -> p q j e", e=2, j=PACK),
                    raw[:].rearrange("p j (q u e) -> p u q j e", u=2, e=2)[:, u],
                )
                quantize_w1(half, 0, a, 2 * u, [P, P] if (a, u) == (1, 0) else [2 * P])

        def stage1(b, t):
            banks = [bank(4 * b + (2 * t + m) % 4, "acc%d%d%d" % (b, t, m)) for m in range(S // BANK)]
            for a in range(2):
                for m in range(S // BANK):
                    cols = slice(BANK * m, BANK * (m + 1))
                    nc.tensor.matmul_mx(
                        out=banks[m][:],
                        lhsT=w1_q[b, a, t][0],
                        lhsT_scale=w1_q[b, a, t][1],
                        rhs=v_words[a][:, cols].bitcast(FP4X4),
                        rhs_scale=v_scales[a][:, cols],
                        start=(a == 0),
                        stop=(a == 1),
                    )
            for m in range(S // BANK):
                cols = slice(BANK * m, BANK * (m + 1))
                bias = b1_sb[:, b, t : t + 1]
                if (b, t, m) == (0, 0, 1):
                    nc.vector.tensor_scalar(h[b][t][:, cols], banks[m][:], bias, None, ALU.add)
                else:
                    nc.scalar.activation(h[b][t][:, cols], banks[m][:], ACT.Identity, bias=bias)

        def pick(b, t, first, second):
            nc.vector.tensor_copy(first[:, t, :], h[b][t][:].indirect(pos1_sb[:]))
            nc.vector.tensor_copy(second[:, t, :], h[b][t][:].indirect(pos2_sb[:]))

        def combine(engine, op, first, second, grouped, parts):
            w = PAIRS // parts
            for c0 in range(0, PAIRS, w):
                engine.tensor_tensor(
                    grouped[:, PACK * c0 : PACK * (c0 + w)].rearrange("p (c i t) -> p c t i", i=2, t=PACK),
                    first[:, :, c0 : c0 + w].rearrange("p t (c i) -> p c t i", i=2),
                    second[:, :, c0 : c0 + w].rearrange("p t (c i) -> p c t i", i=2),
                    op,
                )

        def operand(name):
            return sb([P, PAIRS], U32, name + "_c"), sb([P, PAIRS], U8, name + "_s")

        first0 = sb([P, PACK, PAIRS], F32, "first0")
        second0 = sb([P, PACK, PAIRS], F32, "second0")
        for t in range(PACK - 1):
            stage1(0, t)
            pick(0, t, first0, second0)
        raw10 = load_w1(1, 0, "tab_s")
        raw11 = load_w1(1, 1, "bf_c")
        w1bf_10 = sb([P, KP * PACK], BF16, "w1bf_10", "bf_a")
        cast_w1(raw10, w1bf_10)
        quantize_w1(w1bf_10, 1, 0, 0, [KP])
        stage1(0, PACK - 1)
        pick(0, PACK - 1, first0, second0)
        w1bf_11 = sb([P, KP * PACK], BF16, "w1bf_11", "bf_b")
        cast_w1(raw11, w1bf_11)
        quantize_w1(w1bf_11, 1, 1, 0, [KP])
        for t in range(PACK):
            stage1(1, t)

        peak0_bf = sb([P, PAIRS * PACK], BF16, "peak0_bf", "bf_b")
        combine(nc.vector, ALU.max, first0, second0, peak0_bf, 2)
        peak = [operand("peak0")]
        quantize(peak0_bf, peak[0][0], peak[0][1], [PAIRS // 2] * 2)
        gap0_bf = sb([P, PAIRS * PACK], BF16, "gap0_bf", "bf_b")
        combine(nc.gpsimd, ALU.subtract, first0, second0, gap0_bf, GPSIMD_PARTS)

        w3_scales = [sb([P, N], U8, "w3s%d" % b) for b in range(2)]
        w3_raw = []
        for b in range(2):
            raw = sb([P, PACK, N], F32, "w3raw%d" % b, ("tab_s", "bf_c")[b])
            nc.sync.dma_start(raw[:], w3[KP * b : KP * (b + 1), :].rearrange("(p j) c -> p j c", j=PACK))
            w3_raw.append(raw)
        w2 = sb([P, 6 * N], U8, "w2", "bf_a")
        w2w = w2[:, : 4 * N].rearrange("p (b c) -> p b c", b=2)
        w2s = w2[:, 4 * N :].rearrange("p (b c) -> p b c", b=2)
        nc.sync.dma_start(w2w.bitcast(I32), w2_words.bitcast(I32).rearrange("b p c -> p b c"))
        nc.gpsimd.memset(w2[:, 4 * N :].bitcast(I32), 0)
        w2_rows = w2_scales.bitcast(I32).rearrange("b (q r) c -> r q b c", r=PACK)
        for r in range(PACK):
            nc.sync.dma_start(w2s.bitcast(I32)[r:P:QUAD, :, :], w2_rows[r])
        w3_bf = []
        for b in range(2):
            w3_bf.append(sb([P, N * PACK], BF16, "w3bf_%d" % b))
            for c0, w in ((0, W3_PARTS[0]), (W3_PARTS[0], W3_PARTS[1])):
                nc.scalar.copy(
                    w3_bf[b][:, PACK * c0 : PACK * (c0 + w)].rearrange("p (c i j) -> p c j i", i=2, j=PACK),
                    w3_raw[b][:, :, c0 : c0 + w].rearrange("p j (c i) -> p c j i", i=2),
                )
        b3_sb = sb([P, N // P], F32, "b3_sb", "tab_s")
        with nc.allow_non_contiguous_dma(reason="one bias value for each partition"):
            nc.sync.dma_start(b3_sb[:], b3.rearrange("(i p) -> p i", p=P))

        first1 = sb([P, PACK, PAIRS], F32, "first1")
        second1 = sb([P, PACK, PAIRS], F32, "second1")
        for t in range(PACK):
            pick(1, t, first1, second1)
        late_codes = sb([P, 2 * N + PAIRS], U32, "late_codes", "h13")
        w3_codes = [late_codes[:, N * b : N * (b + 1)] for b in range(2)]
        for b in range(2):
            quantize(w3_bf[b], w3_codes[b], w3_scales[b], W3_PARTS)
        gap = [(late_codes[:, 2 * N :], sb([P, PAIRS], U8, "gap0_s"))]
        quantize(gap0_bf, gap[0][0], gap[0][1], [PAIRS])
        peak1_bf = sb([P, PAIRS * PACK], BF16, "peak1_bf")
        combine(nc.vector, ALU.max, first1, second1, peak1_bf, 2)
        peak.append(operand("peak1"))
        quantize(peak1_bf, peak[1][0], peak[1][1], [PAIRS // 2] * 2)
        gap1_bf = sb([P, PAIRS * PACK], BF16, "gap1_bf")
        combine(nc.vector, ALU.subtract, first1, second1, gap1_bf, 2)
        gap.append(operand("gap1"))
        quantize(gap1_bf, gap[1][0], gap[1][1], [PAIRS // 2] * 2)

        def load_pass(acc, i, b):
            nc.tensor.matmul_mx(
                out=acc[:],
                lhsT=w3_codes[b][:, P * i : P * (i + 1)].bitcast(FP8X4),
                lhsT_scale=w3_scales[b][:, P * i : P * (i + 1)],
                rhs=peak[b][0][:].bitcast(FP8X4),
                rhs_scale=peak[b][1][:],
                start=(b == 0),
                stop=(b == 1),
            )

        def y_pass(acc, i, b):
            nc.tensor.matmul_mx(
                out=acc[:],
                lhsT=w2w[:, b, 2 * P * i : 2 * P * (i + 1)].bitcast(FP4X4),
                lhsT_scale=w2s[:, b, P * i : P * (i + 1)],
                rhs=gap[b][0][:].bitcast(FP8X4),
                rhs_scale=gap[b][1][:],
                start=(b == 0),
                stop=(b == 1),
            )

        tiles = N // P
        load_acc = [bank(i, "load%d" % i) for i in range(tiles)]
        y_acc = [bank(tiles + i, "y%d" % i) for i in range(EARLY_Y)]
        for i in range(tiles):
            load_pass(load_acc[i], i, 0)
        for i in range(EARLY_Y):
            y_pass(y_acc[i], i, 0)
        weight = []
        for i in range(tiles):
            load_pass(load_acc[i], i, 1)
            weight.append(sb([P, PAIRS], F32, "weight%d" % i))
            nc.scalar.activation(weight[i][:], load_acc[i][:], ACT.Tanh, bias=b3_sb[:, i : i + 1])
        for i in range(tiles):
            if i >= EARLY_Y:
                y_acc.append(bank(tiles + i, "y%d" % i))
                y_pass(y_acc[i], i, 0)
            y_pass(y_acc[i], i, 1)
            res = sb([P, PAIRS], F32, "res%d" % i)
            nc.vector.tensor_tensor(res[:], y_acc[i][:], weight[i][:], ALU.mult)
            nc.sync.dma_start(out[P * i : P * (i + 1), :], res[:])
